import numpy as np
import ml_dtypes


def mxq(x, axis, fmt="e4m3"):
    dtype, down = {"e4m3": (ml_dtypes.float8_e4m3fn, 7), "e5m2": (ml_dtypes.float8_e5m2, 14)}[fmt]
    v = np.moveaxis(np.asarray(x, np.float32).astype(ml_dtypes.bfloat16).astype(np.float64), axis, -1)
    blocks = v.reshape(v.shape[:-1] + (-1, 32))
    amax = np.abs(blocks).max(-1, keepdims=True)
    byte = np.maximum(np.where(amax > 0, np.frexp(amax)[1] - 1 + 127, 0) - down, 1)
    scale = np.exp2(byte - 127.0)
    codes = (blocks / scale).astype(np.float32).astype(dtype).astype(np.float64)
    return np.moveaxis((codes * scale).reshape(v.shape), -1, axis)


WIDE = False


def mx_kscale(k):
    if not WIDE:
        return np.ones(k)
    levels = np.array([10, -10, 5, -5, 0])
    if k % 512:
        return np.exp2(np.random.permutation(np.resize(levels, k // 32))).repeat(32)
    a = np.empty((k // 512, 16))
    for p in range(k // 512):
        a[p, :8] = np.random.permutation(np.resize(levels, 8))
        for g in range(8):
            far = levels[np.abs(levels - a[p, g]) >= 10]
            a[p, g + 8] = far[np.random.randint(len(far))]
    return np.exp2(a.ravel()).repeat(32)


def f64(x):
    return np.asarray(x).astype(np.float64)


def striped(idx):
    return np.tile(idx.reshape(-1, 16).T, (8, 1)).astype(np.uint16)


def unstriped(offs):
    return offs[:16].T.reshape(-1).astype(np.int64)


def striped8(idx):
    return np.concatenate([x.reshape(-1, 16).T for x in idx]).astype(np.uint16)


def runs(offs, k):
    lists = np.stack([offs[16 * r : 16 * r + 16].T.reshape(-1) for r in range(8)]).astype(np.int64)
    return lists[np.arange(k) % 512 // 64]


def pack_weight(w):
    k, n = w.shape
    w = f64(np.asarray(w, np.float32).astype(ml_dtypes.bfloat16)).reshape(k // 32, 32, n)
    amax = np.abs(w).max(1)
    byte = np.clip(np.where(amax > 0, np.frexp(amax)[1] - 1 + 127 - 7, 1), 1, 254)
    scaled = (w * np.exp2(127.0 - byte)[:, None, :]).reshape(k, n).astype(np.float32)
    words = np.ascontiguousarray(scaled.reshape(k // 512, 128, 4, n).transpose(0, 1, 3, 2)).astype(ml_dtypes.float8_e4m3fn).view(np.uint8)
    return words, np.ascontiguousarray(byte.astype(np.uint8).reshape(k // 512, 16, n))


def unpack_weight(words, scales):
    g, p, n, _ = words.shape
    vals = np.ascontiguousarray(words).view(ml_dtypes.float8_e4m3fn).astype(np.float64) * np.repeat(np.exp2(scales.astype(np.float64) - 127.0), 8, axis=1)[..., None]
    return vals.transpose(0, 1, 3, 2).reshape(g * 512, n)


K, T, S, V, H, C = 512, 2048, 512, 256, 512, 512


def setup_inputs():
    n = np.random.standard_normal
    s = mx_kscale(K)[:, None]
    packed_xT = pack_weight(n((K, T)) * s)
    return {
        "x_words": packed_xT[0],
        "x_scales": packed_xT[1],
        "w1": (n((K, H)) / np.sqrt(K) / s).astype(np.float32),
        "w2": (n((K, H)) / np.sqrt(K) / s).astype(np.float32),
        "gs": (np.random.uniform(0.5, 1.5, (K, 1)) / s).astype(np.float32),
        "offs": striped(np.random.permutation(T)[:S]),
        "two": striped(np.random.permutation(T)[:S]),
        "sub_l": striped8(np.stack([np.random.permutation(S)[:V] for _ in range(8)])),
        "enz": striped8(np.stack([np.random.permutation(S)[:V] for _ in range(8)])),
        "inh": striped8(np.stack([np.random.permutation(S)[:V] for _ in range(8)])),
        "cand": striped(np.random.permutation(T)[:C]),
    }


def reference(x_words, x_scales, w1, w2, gs, offs, two, sub_l, enz, inh, cand):
    x_cand = unpack_weight(x_words, x_scales)[:, unstriped(cand)]
    xq = unpack_weight(x_words, x_scales)[:, unstriped(offs)]
    y = mxq(f64(w1), 0, "e4m3").T @ xq
    x_two = unpack_weight(x_words, x_scales)[:, unstriped(two)]
    c = ((mxq(f64(w2), 0, "e4m3").T @ x_two)) ** 2
    sb = c[np.arange(H)[:, None], runs(sub_l, H)]
    z = f64(gs) * (((y[np.arange(H)[:, None], runs(enz, H)]) * sb) / (sb + 0.5 + c[np.arange(H)[:, None], runs(inh, H)]))
    return 0.0625 * ((x_cand.T @ mxq(z, 0, "e4m3")))

from contextlib import ExitStack

import concourse.mybir as mybir

K, T, S, V, H, C = 512, 2048, 512, 256, 512, 512
FLOPS = 2 * K * H * S * 2 + 2 * K * C * V

F32 = mybir.dt.float32
BF16 = mybir.dt.bfloat16
I32 = mybir.dt.int32
U32 = mybir.dt.uint32
U16 = mybir.dt.uint16
U8 = mybir.dt.uint8
FP8X4 = mybir.dt.float8_e4m3fn_x4
ACT = mybir.ActivationFunctionType
ALU = mybir.AluOpType

P = 128
PACK = 4
HALF = V // 2


def tile_picked_enzyme_none_p_kernel(tc, x_words, x_scales, w1, w2, gs, offs, two, sub_l, enz, inh, cand, out):
    nc = tc.nc
    with ExitStack() as ctx:
        lists = ctx.enter_context(tc.tile_pool(name="lists", bufs=1))
        keep = ctx.enter_context(tc.tile_pool(name="keep", bufs=1))
        psum = ctx.enter_context(tc.psum_pool(name="psum", bufs=1))

        def load_list(name, src):
            tile = lists.tile(list(src.shape), U16, name=name)
            nc.sync.dma_start(tile[:], src)
            return tile

        def load_weight(name, w):
            halves = []
            for h in range(2):
                raw = keep.tile([P, PACK, H // 2], F32, name="%s_raw%d" % (name, h), tag="%s_raw%d" % (name, h))
                nc.sync.dma_start(raw[:], w.rearrange("(p j) c -> p j c", j=PACK)[:, :, h * (H // 2) : (h + 1) * (H // 2)])
                halves.append(raw)
            return halves

        table_scales = keep.tile([P, T], U8, name="table_scales", align_bytes=64)
        nc.gpsimd.memset(table_scales[:].bitcast(I32), 0)
        two_t = load_list("two_t", two)
        for q in range(4):
            nc.sync.dma_start(table_scales[32 * q : 32 * q + 4, :].bitcast(I32), x_scales[0, 4 * q : 4 * q + 4, :].bitcast(I32))
        offs_t = load_list("offs_t", offs)
        cand_t = load_list("cand_t", cand)
        w2_raw = load_weight("w2", w2)
        table_words = keep.tile([P, T], U32, name="table_words", align_bytes=64)
        nc.sync.dma_start(table_words[:].bitcast(I32), x_words[0].rearrange("p n t -> p (n t)").bitcast(I32))
        sub_t = load_list("sub_t", sub_l)
        inh_t = load_list("inh_t", inh)
        w1_raw = load_weight("w1", w1)
        enz_t = load_list("enz_t", enz)
        gs_t = keep.tile([P, PACK], F32, name="gs_t")
        nc.sync.dma_start(gs_t[:], gs.rearrange("(p t) o -> p (t o)", t=PACK))

        warm = keep.tile([P, 2], F32, name="warm")
        nc.vector.memset(warm[:, 0:1], 1.0)
        nc.scalar.activation(warm[:, 1:2], warm[:, 0:1], ACT.Abs_reciprocal_sqrt)

        def pick(name, table, dtype, index):
            picked = keep.tile([P, S], dtype, name=name, align_bytes=64)
            nc.vector.tensor_copy(picked[:], table[:].indirect(index[:]))
            return picked

        def round_half(grouped, raw, h):
            nc.scalar.copy(
                grouped[:, :, h * (P // 2) : (h + 1) * (P // 2), :].rearrange("p t m j -> p m j t"),
                raw[h][:].rearrange("p j (m t) -> p m j t", t=PACK),
            )

        def quantise(name, grouped, width):
            codes = keep.tile([P, width], U32, name=name + "_codes", align_bytes=64)
            scales = keep.tile([P, width], U8, name=name + "_scales", align_bytes=64)
            nc.vector.quantize_mx(out=codes[:].bitcast(FP8X4), scales=scales[:], in_=grouped)
            return codes, scales

        def product(acc, lhs, cols, rhs):
            nc.tensor.matmul_mx(
                out=acc,
                lhsT=lhs[0][:, cols].bitcast(FP8X4),
                lhsT_scale=lhs[1][:, cols],
                rhs=rhs[0][:].bitcast(FP8X4),
                rhs_scale=rhs[1][:],
                start=True,
                stop=True,
            )

        def bank(b, shape):
            return psum.tile(shape, F32, name="acc", tag="bank%d" % b)

        two_scales = pick("two_scales", table_scales, U8, two_t)
        offs_scales = pick("offs_scales", table_scales, U8, offs_t)
        cand_scales = pick("cand_scales", table_scales, U8, cand_t)
        w2_grouped = keep.tile([P, PACK, P, PACK], BF16, name="w2_grouped", align_bytes=64)
        round_half(w2_grouped, w2_raw, 0)
        round_half(w2_grouped, w2_raw, 1)
        w2_mx = quantise("w2", w2_grouped[:].rearrange("p t m j -> p (t m j)"), H)
        two_words = pick("two_words", table_words, U32, two_t)
        offs_words = pick("offs_words", table_words, U32, offs_t)
        cand_words = pick("cand_words", table_words, U32, cand_t)

        w1_grouped = keep.tile([P, PACK, P, PACK], BF16, name="w1_grouped", tag="w1_grouped", align_bytes=64)
        conc = []

        def square(t, tag):
            acc = bank(t, [P, S])
            product(acc[:], w2_mx, slice(t * P, (t + 1) * P), (two_words, two_scales))
            c_t = keep.tile([P, S], F32, name="conc%d" % t, tag=tag)
            nc.scalar.activation(c_t[:], acc[:], ACT.Square)
            conc.append(c_t)

        round_half(w1_grouped, w1_raw, 0)
        square(0, "w1_raw0")
        square(1, "conc1")
        round_half(w1_grouped, w1_raw, 1)
        square(2, "w1_raw1")
        square(3, "conc3")

        substrate = []
        total = keep.tile([P, PACK, V], F32, name="total")

        def fetch_conc(t, tag):
            sb = keep.tile([P, V], F32, name="substrate%d" % t, tag=tag, align_bytes=64)
            nc.vector.tensor_copy(sb[:], conc[t][:].indirect(sub_t[:]))
            nc.vector.tensor_tensor(total[:, t, :], conc[t][:].indirect(inh_t[:]), sb[:], ALU.add)
            substrate.append(sb)

        fetch_conc(0, "substrate0")
        fetch_conc(1, "substrate1")
        w1_mx = quantise("w1", w1_grouped[:].rearrange("p t m j -> p (t m j)"), H)
        fetch_conc(2, "w1_grouped")
        fetch_conc(3, "substrate3")

        speed = []
        for t in range(PACK):
            acc = bank(PACK + t, [P, S])
            product(acc[:], w1_mx, slice(t * P, (t + 1) * P), (offs_words, offs_scales))
            y_t = keep.tile([P, S], F32, name="speed%d" % t)
            nc.scalar.activation(y_t[:], acc[:], ACT.Copy, scale=gs_t[:, t : t + 1])
            speed.append(y_t)
        root = keep.tile([P, PACK, V], F32, name="root")
        inverse = keep.tile([P, PACK, V], F32, name="inverse")
        nc.scalar.activation(root[:], total[:], ACT.Abs_reciprocal_sqrt, bias=0.5)
        nc.scalar.activation(inverse[:], root[:], ACT.Square)

        for h in range(2):
            cols = slice(h * HALF, (h + 1) * HALF)
            rate = keep.tile([P, PACK, HALF], F32, name="rate%d" % h)
            for t in range(PACK):
                nc.vector.tensor_tensor(rate[:, t, :], speed[t][:].indirect(enz_t[:, h * (HALF // 16) : (h + 1) * (HALF // 16)]), substrate[t][:, cols], ALU.mult)
            z = keep.tile([P, HALF, PACK], BF16, name="z%d" % h, align_bytes=64)
            nc.vector.tensor_tensor(
                z[:].rearrange("p (c i) t -> p c t i", i=4),
                rate[:].rearrange("p t (c i) -> p c t i", i=4),
                inverse[:, :, cols].rearrange("p t (c i) -> p c t i", i=4),
                ALU.mult,
            )
            z_mx = quantise("z%d" % h, z[:].rearrange("p v t -> p (v t)"), HALF)
            for pair in range(2):
                acc = bank(2 * h + pair, [P, 2, HALF])
                for m in range(2):
                    first = (2 * pair + m) * P
                    product(acc[:, m, :], (cand_words, cand_scales), slice(first, first + P), z_mx)
                score = keep.tile([P, 2, HALF], F32, name="score%d%d" % (h, pair))
                if h == 1 and pair == 1:
                    nc.vector.tensor_scalar_mul(score[:], acc[:], 0.0625)
                else:
                    nc.scalar.mul(score[:], acc[:], 0.0625)
                nc.sync.dma_start(out.rearrange("(m p) v -> p m v", p=P)[:, 2 * pair : 2 * pair + 2, cols], score[:])
